import numpy as np
import ml_dtypes


def mxq(x, axis, fmt="e4m3"):
    dtype, down = {"e4m3": (ml_dtypes.float8_e4m3fn, 7), "e5m2": (ml_dtypes.float8_e5m2, 14)}[fmt]
    v = np.moveaxis(np.asarray(x, np.float32).astype(ml_dtypes.bfloat16).astype(np.float64), axis, -1)
    blocks = v.reshape(v.shape[:-1] + (-1, 32))
    amax = np.abs(blocks).max(-1, keepdims=True)
    byte = np.maximum(np.where(amax > 0, np.frexp(amax)[1] - 1 + 127, 0) - down, 1)
    scale = np.exp2(byte - 127.0)
    codes = (blocks / scale).astype(np.float32).astype(dtype).astype(np.float64)
    return np.moveaxis((codes * scale).reshape(v.shape), -1, axis)


WIDE = False


def mx_kscale(k):
    if not WIDE:
        return np.ones(k)
    levels = np.array([10, -10, 5, -5, 0])
    if k % 512:
        return np.exp2(np.random.permutation(np.resize(levels, k // 32))).repeat(32)
    a = np.empty((k // 512, 16))
    for p in range(k // 512):
        a[p, :8] = np.random.permutation(np.resize(levels, 8))
        for g in range(8):
            far = levels[np.abs(levels - a[p, g]) >= 10]
            a[p, g + 8] = far[np.random.randint(len(far))]
    return np.exp2(a.ravel()).repeat(32)


def f64(x):
    return np.asarray(x).astype(np.float64)


def striped(idx):
    return np.tile(idx.reshape(-1, 16).T, (8, 1)).astype(np.uint16)


def unstriped(offs):
    return offs[:16].T.reshape(-1).astype(np.int64)


def striped8(idx):
    return np.concatenate([x.reshape(-1, 16).T for x in idx]).astype(np.uint16)


def runs(offs, k):
    lists = np.stack([offs[16 * r : 16 * r + 16].T.reshape(-1) for r in range(8)]).astype(np.int64)
    return lists[np.arange(k) % 512 // 64]


def pack_weight(w):
    k, n = w.shape
    w = f64(np.asarray(w, np.float32).astype(ml_dtypes.bfloat16)).reshape(k // 32, 32, n)
    amax = np.abs(w).max(1)
    byte = np.clip(np.where(amax > 0, np.frexp(amax)[1] - 1 + 127 - 7, 1), 1, 254)
    scaled = (w * np.exp2(127.0 - byte)[:, None, :]).reshape(k, n).astype(np.float32)
    words = np.ascontiguousarray(scaled.reshape(k // 512, 128, 4, n).transpose(0, 1, 3, 2)).astype(ml_dtypes.float8_e4m3fn).view(np.uint8)
    return words, np.ascontiguousarray(byte.astype(np.uint8).reshape(k // 512, 16, n))


def unpack_weight(words, scales):
    g, p, n, _ = words.shape
    vals = np.ascontiguousarray(words).view(ml_dtypes.float8_e4m3fn).astype(np.float64) * np.repeat(np.exp2(scales.astype(np.float64) - 127.0), 8, axis=1)[..., None]
    return vals.transpose(0, 1, 3, 2).reshape(g * 512, n)

def planes(y):
    n, m = y.shape
    v = y.astype(np.float32).astype(ml_dtypes.bfloat16).astype(np.float64).reshape(n // 32, 32, m)
    top = np.abs(v).max(1)
    byte = np.clip(np.where(top > 0, np.frexp(top)[1] - 1 + 127 - 7, 1), 1, 254)
    codes = (v * np.exp2(127.0 - byte)[:, None, :]).reshape(n, m).astype(np.float32).astype(ml_dtypes.float8_e4m3fn).view(np.uint8)
    words = codes.reshape(n // 512, 128, 4, m).transpose(0, 1, 3, 2)
    return np.ascontiguousarray(words), np.ascontiguousarray(byte.astype(np.uint8).reshape(n // 512, 16, m))


K, T, S, N, H, W, U = 512, 2048, 512, 512, 512, 256, 1024


def setup_inputs():
    n = np.random.standard_normal
    s = mx_kscale(K)[:, None]
    u = mx_kscale(H)
    packed_xT = pack_weight(n((K, T)) * s)
    packed_w3 = pack_weight(n((H, N)) / np.sqrt(H) / u[:, None])
    perm = np.stack([np.random.permutation(S) for _ in range(8)])
    return {
        "x_words": packed_xT[0],
        "x_scales": packed_xT[1],
        "w1": (n((K, H)) / np.sqrt(K) / s * u).astype(np.float32),
        "w2": (n((H, H)) / np.sqrt(H) / u[:, None] * u).astype(np.float32),
        "mem": (n((H, U)) * u[:, None]).astype(np.float32),
        "w3_words": packed_w3[0],
        "w3_scales": packed_w3[1],
        "res": n((N, U)).astype(np.float32),
        "offs": striped(np.random.permutation(T)[:S]),
        "n1": striped8(perm[:, :W]),
        "n2": striped8(perm[:, W:]),
        "n3": striped8(np.stack([np.random.permutation(U)[:S] for _ in range(8)])),
        "n4": striped8(np.stack([np.random.permutation(U) for _ in range(8)])),
    }


def reference(x_words, x_scales, w1, w2, mem, w3_words, w3_scales, res, offs, n1, n2, n3, n4):
    xq = unpack_weight(x_words, x_scales)[:, unstriped(offs)]
    y = mxq(f64(w1), 0, "e4m3").T @ xq
    pa = y[np.arange(H)[:, None], runs(n1, H)]
    pb = y[np.arange(H)[:, None], runs(n2, H)]
    rb = np.minimum(pa, pb)
    ra = np.maximum(pa, pb)
    ds = np.zeros((H, S))
    ds[np.arange(H)[:, None], runs(n1, H)] = ra
    z = ds.copy()
    z[np.arange(H)[:, None], runs(n2, H)] = rb
    h = mxq(f64(w2), 0, "e4m3").T @ mxq(z, 0, "e4m3")
    pg = f64(mem).copy()
    pg[np.arange(H)[:, None], runs(n3, H)] = h
    z2 = pg - (0.5 * (pg[np.arange(H)[:, None], runs(n4, H)]))
    out_0 = f64(res) + (unpack_weight(w3_words, w3_scales).T @ mxq(z2, 0, "e4m3"))
    return (out_0,) + planes(out_0)

from contextlib import ExitStack

import concourse.mybir as mybir

F32 = mybir.dt.float32
BF16 = mybir.dt.bfloat16
I32 = mybir.dt.int32
U32 = mybir.dt.uint32
U16 = mybir.dt.uint16
U8 = mybir.dt.uint8
FP8X4 = mybir.dt.float8_e4m3fn_x4
ALU = mybir.AluOpType
COPY = mybir.ActivationFunctionType.Copy

P = 128
PACK = 4
T, S, W, U, H = 2048, 512, 256, 1024, 512
HALF = S // 2
CHUNK = 256
CHUNKS = U // CHUNK
FLOPS = 2 * H * H * S * 2 + 2 * H * H * U


def tile_picked_deeporderpagem_none_po_kernel(
    tc, x_words, x_scales, w1, w2, mem, w3_words, w3_scales, res, offs, n1, n2, n3, n4, out_0, out_1, out_2
):
    nc = tc.nc
    with ExitStack() as ctx:
        keep = ctx.enter_context(tc.tile_pool(name="keep", bufs=1))
        late = ctx.enter_context(tc.tile_pool(name="late", bufs=1))
        psum = ctx.enter_context(tc.psum_pool(name="psum", bufs=8))

        def sb(name, shape, dtype):
            return keep.tile(shape, dtype, name=name, align_bytes=64)

        def bank():
            return psum.tile([P, 512], F32, name="bank")

        def load_list(name, src):
            lst = keep.tile(list(src.shape), U16, name=name)
            nc.sync.dma_start(lst[:], src)
            return lst

        def load_scale_rows(queue, name, src, width):
            rows = sb(name, [P, width], U8)
            nc.gpsimd.memset(rows[:].bitcast(I32), 0)
            for q in range(4):
                queue.dma_start(rows[32 * q : 32 * q + 4, :].bitcast(I32), src[0, 4 * q : 4 * q + 4, :].bitcast(I32))
            return rows

        def load_weight(name, src):
            halves = []
            for u in range(2):
                raw = sb(f"{name}_raw{u}", [P, PACK, H // 2], F32)
                nc.sync.dma_start(raw[:], src.rearrange("(p j) c -> p j c", j=PACK)[:, :, u * (H // 2) : (u + 1) * (H // 2)])
                halves.append(raw)
            return halves

        def round_weight(copy, grouped, raw, u):
            dst = grouped[:].rearrange("p (t m j) -> p m t j", t=PACK, j=PACK)[:, 64 * u : 64 * (u + 1), :, :]
            copy(dst, raw[:].rearrange("p j (m t) -> p m t j", t=PACK))

        def quantize(codes, scales, grouped):
            nc.vector.quantize_mx(out=codes.bitcast(FP8X4), scales=scales, in_=grouped)

        def product(out, w_codes, w_scales, t, codes, scales):
            cols = slice(t * P, (t + 1) * P)
            nc.tensor.matmul_mx(
                out=out, lhsT=w_codes[:, cols].bitcast(FP8X4), lhsT_scale=w_scales[:, cols],
                rhs=codes.bitcast(FP8X4), rhs_scale=scales, start=True, stop=True,
            )

        def interleave(copy, grouped, planes):
            copy(grouped.rearrange("p (c i t) -> p c t i", i=4, t=PACK), planes.rearrange("p t (c i) -> p c t i", i=4))

        offs_t = load_list("offs", offs)
        xs = load_scale_rows(nc.sync, "xs", x_scales, T)
        w1_raw = load_weight("w1", w1)
        xw = sb("xw", [P, T], I32)
        nc.sync.dma_start(xw[:], x_words[0].rearrange("p n t -> p (n t)").bitcast(I32))
        n1_t = load_list("n1", n1)
        n2_t = load_list("n2", n2)
        w2_raw = load_weight("w2", w2)
        n3_t = load_list("n3", n3)
        n4_t = load_list("n4", n4)
        w3w_raw = sb("w3w_raw", [P, H], I32)
        nc.sync.dma_start(w3w_raw[:], w3_words[0].rearrange("p n t -> p (n t)").bitcast(I32))
        w3s_raw = load_scale_rows(nc.sync, "w3s_raw", w3_scales, H)
        pg = []
        for t in range(PACK):
            page = sb(f"pg{t}", [P, U], F32)
            nc.sync.dma_start(page[:], mem.rearrange("(p t) w -> p t w", t=PACK)[:, t, :])
            pg.append(page)
        res_t = sb("res", [P, PACK, U], F32)
        nc.sync.dma_start(res_t[:], res.rearrange("(p t) w -> p t w", t=PACK))

        xs_g = sb("xs_g", [P, S], U8)
        nc.vector.tensor_copy(xs_g[:], xs[:].indirect(offs_t[:]))
        w1_bf = sb("w1_bf", [P, PACK * H], BF16)
        round_weight(nc.scalar.copy, w1_bf, w1_raw[0], 0)
        round_weight(nc.vector.tensor_copy, w1_bf, w1_raw[1], 1)
        w1_c = sb("w1_c", [P, H], U32)
        w1_s = sb("w1_s", [P, H], U8)
        quantize(w1_c[:], w1_s[:], w1_bf[:])
        xw_g = sb("xw_g", [P, S], U32)
        for u in range(2):
            nc.vector.tensor_copy(
                xw_g[:, u * HALF : (u + 1) * HALF], xw[:].bitcast(U32).indirect(offs_t[:, 16 * u : 16 * (u + 1)])
            )
        y = [sb(f"y{t}", [P, S], F32) for t in range(PACK)]
        for t in range(PACK):
            for u in range(2):
                cols = slice(u * HALF, (u + 1) * HALF)
                acc = bank()
                product(acc[:, :HALF], w1_c, w1_s, t, xw_g[:, cols], xs_g[:, cols])
                nc.scalar.copy(y[t][:, cols], acc[:, :HALF])

        w2_bf = sb("w2_bf", [P, PACK * H], BF16)
        for u in range(2):
            round_weight(nc.scalar.copy, w2_bf, w2_raw[u], u)

        z = [sb(f"z{t}", [P, S], F32) for t in range(PACK)]
        z_bf = sb("z_bf", [P, S, PACK], BF16)
        for pair in range(2):
            ts = (2 * pair, 2 * pair + 1)
            pa, pb, ra, rb = {}, {}, {}, {}
            for t in ts:
                pa[t] = sb(f"pa{t}", [P, W], F32)
                pb[t] = sb(f"pb{t}", [P, W], F32)
                nc.vector.tensor_copy(pa[t][:], y[t][:].indirect(n1_t[:]))
                nc.vector.tensor_copy(pb[t][:], y[t][:].indirect(n2_t[:]))
            for t in ts:
                ra[t] = sb(f"ra{t}", [P, W], F32)
                if t == PACK - 1:
                    rb[t] = late.tile([P, W], F32, name="rb_last", align_bytes=64, offset=4 * H - 64)
                else:
                    rb[t] = sb(f"rb{t}", [P, W], F32)
                nc.vector.tensor_tensor(ra[t][:], pa[t][:], pb[t][:], ALU.max)
                nc.vector.tensor_tensor(rb[t][:], pa[t][:], pb[t][:], ALU.min)
            for t in ts:
                nc.vector.tensor_copy(z[t][:].indirect(n1_t[:]), ra[t][:])
            for t in ts:
                nc.vector.tensor_copy(z[t][:].indirect(n2_t[:]), rb[t][:])
            for t in ts:
                for u in range(2):
                    cols = slice(u * HALF, (u + 1) * HALF)
                    nc.scalar.copy(z_bf[:, cols, t], z[t][:, cols])

        w2_c = sb("w2_c", [P, H], U32)
        w2_s = late.tile([P, H], U8, name="w2_s", align_bytes=64, offset=4 * H)
        quantize(w2_c[:], w2_s[:], w2_bf[:])
        w3_c = late.tile([P, H], I32, name="w3_c", align_bytes=64, offset=0)
        w3_s = late.tile([P, H], U8, name="w3_s", align_bytes=64, offset=5 * H)
        nc.vector.tensor_copy(w3_c[:].rearrange("p (t m) -> p m t", t=PACK), w3w_raw[:].rearrange("p (m t) -> p m t", t=PACK))
        nc.vector.tensor_copy(w3_s[:].rearrange("p (t m) -> p m t", t=PACK), w3s_raw[:].rearrange("p (m t) -> p m t", t=PACK))

        z_c = sb("z_c", [P, S], U32)
        z_s = sb("z_s", [P, S], U8)
        h = [sb(f"h{t}", [P, S], F32) for t in range(PACK)]
        for u in range(2):
            cols = slice(u * HALF, (u + 1) * HALF)
            quantize(z_c[:, cols], z_s[:, cols], z_bf[:, cols, :].rearrange("p c t -> p (c t)"))
        for u in range(2):
            cols = slice(u * HALF, (u + 1) * HALF)
            for t in range(PACK):
                acc = bank()
                product(acc[:, :HALF], w2_c, w2_s, t, z_c[:, cols], z_s[:, cols])
                nc.scalar.copy(h[t][:, cols], acc[:, :HALF])
        for u in range(2):
            cols = slice(u * HALF, (u + 1) * HALF)
            for t in range(PACK):
                nc.vector.tensor_copy(pg[t][:].indirect(n3_t[:, 16 * u : 16 * (u + 1)]), h[t][:, cols])
        neg_half = []
        for t in range(PACK):
            scaled = sb(f"neg_half{t}", [P, U], F32)
            nc.scalar.activation(scaled[:], pg[t][:], COPY, scale=-0.5)
            neg_half.append(scaled)

        o_c = sb("o_c", [P, U], I32)
        o_s = sb("o_s", [P, U], U8)
        z2_bf, sums, o_bf = {}, {}, {}

        def fetch(c):
            cols = slice(c * CHUNK, (c + 1) * CHUNK)
            z2 = sb(f"z2_{c}", [P, PACK, CHUNK], F32)
            for t in range(PACK):
                nc.vector.tensor_tensor(
                    z2[:, t, :], neg_half[t][:].indirect(n4_t[:, 16 * c : 16 * (c + 1)]), pg[t][:, cols], ALU.add
                )
            z2_bf[c] = sb(f"z2_bf{c}", [P, PACK * CHUNK], BF16)
            interleave(nc.scalar.copy, z2_bf[c][:], z2[:])

        def multiply(c):
            codes = sb(f"z2_c{c}", [P, CHUNK], U32)
            scales = sb(f"z2_s{c}", [P, CHUNK], U8)
            quantize(codes[:], scales[:], z2_bf[c][:])
            sums[c] = [bank(), bank()]
            for u in range(2):
                part = slice(u * P, (u + 1) * P)
                for t in range(PACK):
                    product(sums[c][u][:, t * P : (t + 1) * P], w3_c, w3_s, t, codes[:, part], scales[:, part])

        def add_residual(c):
            cols = slice(c * CHUNK, (c + 1) * CHUNK)
            o = sb(f"o{c}", [P, PACK, CHUNK], F32)
            o_bf[c] = sb(f"o_bf{c}", [P, PACK * CHUNK], BF16)
            for u in range(2):
                part = slice(u * P, (u + 1) * P)
                nc.vector.tensor_tensor(
                    o[:, :, part], sums[c][u][:].rearrange("p (t c) -> p t c", t=PACK),
                    res_t[:, :, c * CHUNK + u * P : c * CHUNK + (u + 1) * P], ALU.add,
                )
                copy = nc.vector.tensor_copy if (c, u) == (CHUNKS - 1, 1) else nc.scalar.copy
                interleave(copy, o_bf[c][:, u * PACK * P : (u + 1) * PACK * P], o[:, :, part])
            nc.sync.dma_start(out_0.rearrange("(p t) w -> p t w", t=PACK)[:, :, cols], o[:])

        def hand_on(c):
            cols = slice(c * CHUNK, (c + 1) * CHUNK)
            quantize(o_c[:, cols], o_s[:, cols], o_bf[c][:])
            nc.sync.dma_start(out_1[0].rearrange("p n t -> p (n t)").bitcast(I32)[:, cols], o_c[:, cols])

        stages = (fetch, multiply, add_residual, hand_on)
        for step in range(CHUNKS + len(stages) - 1):
            for lag, stage in enumerate(stages):
                if 0 <= step - lag < CHUNKS:
                    stage(step - lag)
        for q in range(4):
            queue = nc.sync if q % 2 == 0 else nc.scalar
            queue.dma_start(out_2[0, 4 * q : 4 * q + 4, :].bitcast(I32), o_s[32 * q : 32 * q + 4, :].bitcast(I32))
